import numpy as np
import ml_dtypes


def mxq(x, axis, fmt="e4m3"):
    dtype, down = {"e4m3": (ml_dtypes.float8_e4m3fn, 7), "e5m2": (ml_dtypes.float8_e5m2, 14)}[fmt]
    v = np.moveaxis(np.asarray(x, np.float32).astype(ml_dtypes.bfloat16).astype(np.float64), axis, -1)
    blocks = v.reshape(v.shape[:-1] + (-1, 32))
    amax = np.abs(blocks).max(-1, keepdims=True)
    byte = np.maximum(np.where(amax > 0, np.frexp(amax)[1] - 1 + 127, 0) - down, 1)
    scale = np.exp2(byte - 127.0)
    codes = (blocks / scale).astype(np.float32).astype(dtype).astype(np.float64)
    return np.moveaxis((codes * scale).reshape(v.shape), -1, axis)


WIDE = False


def mx_kscale(k):
    if not WIDE:
        return np.ones(k)
    levels = np.array([30, -30])
    if k % 512:
        return np.exp2(np.random.permutation(np.resize(levels, k // 32))).repeat(32)
    a = np.empty((k // 512, 16))
    for p in range(k // 512):
        a[p, :8] = np.random.permutation(np.resize(levels, 8))
        for g in range(8):
            far = levels[np.abs(levels - a[p, g]) >= 10]
            a[p, g + 8] = far[np.random.randint(len(far))]
    return np.exp2(a.ravel()).repeat(32)


BF16 = ml_dtypes.bfloat16


def bf(x):
    return np.asarray(x, np.float32).astype(BF16)


def f64(x):
    return np.asarray(x).astype(np.float64)


E2M1 = np.array([0.0, 0.5, 1.0, 1.5, 2.0, 3.0, 4.0, 6.0, -0.0, -0.5, -1.0, -1.5, -2.0, -3.0, -4.0, -6.0])


def pack_weight(w, fmt):
    k, n = w.shape
    w = f64(bf(w)).reshape(k // 32, 32, n)
    amax = np.abs(w).max(1)
    if fmt in ("e4m3", "e5m2"):
        byte = np.frexp(amax)[1] - 1 + 127 - (7 if fmt == "e4m3" else 14)
    else:
        mant, ex = np.frexp(amax / 6.0)
        byte = np.where(mant > 0.5, ex, ex - 1) + 127
    byte = np.clip(np.where(amax > 0, byte, 1), 1, 254)
    scaled = (w * np.exp2(127.0 - byte)[:, None, :]).reshape(k, n).astype(np.float32)
    by_word = np.ascontiguousarray(scaled.reshape(k // 512, 128, 4, n).transpose(0, 1, 3, 2))
    if fmt in ("e4m3", "e5m2"):
        words = by_word.astype(ml_dtypes.float8_e4m3fn if fmt == "e4m3" else ml_dtypes.float8_e5m2).view(np.uint8)
    else:
        c = by_word.astype(ml_dtypes.float4_e2m1fn).view(np.uint8) & 0xF
        words = c[..., 0::2] | (c[..., 1::2] << 4)
    return np.ascontiguousarray(words), np.ascontiguousarray(byte.astype(np.uint8).reshape(k // 512, 16, n))


def unpack_weight(words, scales, fmt):
    g, p, n, _ = words.shape
    if fmt in ("e4m3", "e5m2"):
        vals = np.ascontiguousarray(words).view(ml_dtypes.float8_e4m3fn if fmt == "e4m3" else ml_dtypes.float8_e5m2).astype(np.float64)
    else:
        nib = np.empty((g, p, n, 4), np.uint8)
        nib[..., 0::2] = words & 0xF
        nib[..., 1::2] = words >> 4
        vals = E2M1[nib]
    vals = vals * np.repeat(np.exp2(scales.astype(np.float64) - 127.0), 8, axis=1)[..., None]
    return vals.transpose(0, 1, 3, 2).reshape(g * 512, n)

def planes(Y):
    n, m = Y.shape
    b = f64(bf(Y)).reshape(n // 32, 32, m)
    amax = np.abs(b).max(1)
    byte = np.clip(np.where(amax > 0, np.frexp(amax)[1] - 1 + 127 - 7, 1), 1, 254)
    codes = (b * np.exp2(127.0 - byte)[:, None, :]).reshape(n, m).astype(np.float32).astype(ml_dtypes.float8_e4m3fn).view(np.uint8)
    words = codes.reshape(n // 512, 128, 4, m).transpose(0, 1, 3, 2)
    return np.ascontiguousarray(words), np.ascontiguousarray(byte.astype(np.uint8).reshape(n // 512, 16, m))


T, R, J, NB = 2, 1024, 2048, 1024
SIGMA = 0.25
MU_TOP, MU_LOW = 0.3, -0.3

def setup_inputs():
    rn = np.random.randn
    s = mx_kscale(NB)
    g = 0.4 * rn(T * R, NB) / np.exp(rn(T * R, NB))
    g_words, g_scales = pack_weight((g * s).T, "e5m2")
    w = np.exp(0.8 * rn(J))
    blocks = 0.25 * w[:, None] * np.exp(rn(J, NB)) / np.sqrt(NB)
    c = np.cos(0.5 * np.pi + 0.4 * rn(R, J))
    d = c - np.linspace(MU_TOP, MU_LOW, T)[:, None, None]
    slope = -d / SIGMA ** 2 * np.exp(-0.5 * d ** 2 / SIGMA ** 2)
    run = 0.5 * w * rn(R, J)
    return {"g_words": g_words, "g_scales": g_scales, "blocks": bf(blocks / s),
            "slope": bf(slope), "run": bf(run)}

def reference(g_words, g_scales, blocks, slope, run):
    h = unpack_weight(g_words, g_scales, "e5m2")
    bq = mxq(f64(blocks), 1, "e4m3")
    p = (h.T @ bq.T).reshape(T, R, J)
    sl = f64(slope)
    y = f64(run) + p[0] * sl[0] + p[1] * sl[1]
    Y = y.T
    words, scales = planes(Y)
    return y, words, scales

@@ -1,0 +1,383 @@
+from contextlib import ExitStack
+
+import concourse.mybir as mybir
+from concourse.masks import make_identity
+
+T, R, J, NB = 2, 1024, 2048, 1024
+FLOPS = 2 * T * R * J * NB
+
+F32 = mybir.dt.float32
+BF16 = mybir.dt.bfloat16
+U32 = mybir.dt.uint32
+I32 = mybir.dt.int32
+U8 = mybir.dt.uint8
+E4M3X4 = mybir.dt.float8_e4m3fn_x4
+E5M2X4 = mybir.dt.float8_e5m2_x4
+ADD = mybir.AluOpType.add
+MULT = mybir.AluOpType.mult
+
+P = 128
+GROUP = 512
+PASSES = NB // GROUP
+CHUNK = 256
+UNIT_R = 256
+UNIT_J = 1024
+UNIT = 2048
+R_UNITS = R // UNIT_R
+UNITS = R_UNITS * (J // UNIT_J)
+BANKS = 8
+POOL_COLS = 1792
+POOL_COLS_LAST = 832
+
+
+def tile_kernel_bin_similarity_gradient_k2_kernel(
+    tc, g_words, g_scales, blocks, slope, run, out_0, out_1, out_2
+):
+    nc = tc.nc
+    with ExitStack() as ctx:
+        keep = ctx.enter_context(tc.tile_pool(name="keep", bufs=1))
+        ring = ctx.enter_context(tc.tile_pool(name="ring", bufs=2))
+        psum = ctx.enter_context(tc.psum_pool(name="psum", bufs=1))
+        ctx.enter_context(tc.manual_schedule())
+
+        ident = keep.tile([P, P], F32, name="ident")
+        make_identity(nc, ident[:])
+        h_scales = keep.tile([P, PASSES * T * R], U8, name="h_scales", align_bytes=64)
+        nc.vector.memset(h_scales[:].bitcast(U32), 0)
+
+        h_words = {}
+        raw = {}
+        sorted_words = {}
+        slope_sb = {}
+        run_sb = {}
+        b_grouped = {}
+        b_codes = {}
+        b_scales = {}
+        prod = {}
+        part = {}
+        y_sb = {}
+        y_bf = {}
+        y_grouped = {}
+        mx_bank = {}
+
+        y_codes = {}
+        first_unit = [0, 0, 0, 0, 4, 4, 6, 7]
+        for i0 in sorted(set(first_unit)):
+            width = first_unit.count(i0) * UNIT_R
+            y_codes[i0] = keep.tile([P, 2, width], U32, name="y_codes%d" % i0, align_bytes=64)
+        y_scales = [keep.tile([P, 2, R], U8, name="y_scales%d" % h, align_bytes=64) for h in range(2)]
+
+        def rows_of(i):
+            return (i % R_UNITS) * UNIT_R
+
+        def cols_of(i):
+            return (i // R_UNITS) * UNIT_J
+
+        def unit_view(dram, i):
+            r0, j0 = rows_of(i), cols_of(i)
+            return dram[r0 : r0 + UNIT_R, j0 : j0 + UNIT_J].rearrange("(t p) j -> p t j", p=P)
+
+        def load_blocks(c):
+            raw[c] = ring.tile([P, 2 * NB], BF16, name="raw", bufs=4, align_bytes=64)
+            nc.sync.dma_start(
+                out=raw[c][:],
+                in_=blocks[c * CHUNK : (c + 1) * CHUNK, :].rearrange("(p s) k -> p (s k)", s=2),
+            )
+
+        def load_h_scales():
+            for q in range(4):
+                nc.sync.dma_start(
+                    out=h_scales[32 * q : 32 * q + 4, :].bitcast(I32).rearrange("r (g n) -> r g n", g=PASSES),
+                    in_=g_scales[:, 4 * q : 4 * q + 4, :].rearrange("g r n -> r g n").bitcast(I32),
+                )
+
+        def load_h_words(i, a):
+            h_words[i, a] = keep.tile([P, PASSES, UNIT_R], U32, name="h_words%d%d" % (i, a), align_bytes=64)
+            n0 = a * R + rows_of(i)
+            nc.sync.dma_start(
+                out=h_words[i, a][:].bitcast(I32),
+                in_=g_words.rearrange("g p n t -> p g (n t)")[:, :, 4 * n0 : 4 * (n0 + UNIT_R)].bitcast(I32),
+            )
+
+        def load_slope(i, a):
+            slope_sb[i, a] = ring.tile([P, UNIT], BF16, name="slope%d" % a, bufs=5 - a)
+            nc.sync.dma_start(out=slope_sb[i, a][:].rearrange("p (t j) -> p t j", t=2), in_=unit_view(slope[a], i))
+
+        def load_run(i):
+            run_sb[i] = ring.tile([P, UNIT], BF16, name="run", bufs=4)
+            nc.sync.dma_start(out=run_sb[i][:].rearrange("p (t j) -> p t j", t=2), in_=unit_view(run, i))
+
+        def load_first(i):
+            if i < R_UNITS:
+                load_h_words(i, 0)
+            load_slope(i, 0)
+
+        def load_second(i):
+            if i < R_UNITS:
+                load_h_words(i, 1)
+            load_slope(i, 1)
+            load_run(i)
+
+        stream = []
+        busy = [False] * BANKS
+        issued = [0]
+
+        def pump():
+            while issued[0] < len(stream):
+                item = stream[issued[0]]
+                b = issued[0] % BANKS
+                if busy[b] or not item[0]():
+                    break
+                bank = psum.tile([P, GROUP], F32, name="bank%d" % b)
+                issued[0] = issued[0] + 1
+                item[1](bank, b)
+
+        def sort_blocks(c):
+            sorted_words[c] = ring.tile([P, NB], F32, name="sorted_words", tag="y", bufs=4)
+            nc.vector.tensor_copy(
+                out=sorted_words[c][:].rearrange("p (x u w) -> p x u w", x=4, u=2),
+                in_=raw[c][:].bitcast(F32).rearrange("p (x w u) -> p x u w", x=4, u=2),
+            )
+            pump()
+
+        def turn_blocks(c, kp):
+            def ready():
+                return c in (sorted_words if c < 4 else raw)
+
+            def emit(bank, b):
+                for s in range(2):
+                    for u in range(2):
+                        w0 = s * (NB // 2) + kp * 256
+                        if c < 4:
+                            words = sorted_words[c][:, w0 + u * P : w0 + (u + 1) * P]
+                        else:
+                            words = raw[c][:].bitcast(F32)[:, w0 + u : w0 + 256 : 2]
+                        nc.tensor.transpose(bank[:, (2 * s + u) * P : (2 * s + u + 1) * P], words, ident[:])
+                key = (c // 2, kp)
+                if key not in b_grouped:
+                    b_grouped[key] = ring.tile([P, 4 * GROUP], BF16, name="b_grouped", bufs=4, align_bytes=64)
+                dst = b_grouped[key][:].bitcast(F32)[:, (c % 2) * GROUP : (c % 2 + 1) * GROUP]
+                dst = dst.rearrange("q (p x) -> q p x", x=4)
+                src = bank[:].rearrange("q (x p) -> q p x", x=4)
+                nc.scalar.copy(out=dst, in_=src)
+
+            return (ready, emit)
+
+        def multiply(i, a, k):
+            rt, jl = k % 2, k // 2
+            jg = cols_of(i) // GROUP + jl
+
+            def ready():
+                return all((jg, kp) in b_codes for kp in range(PASSES)) and (i % R_UNITS, a) in h_words
+
+            def emit(bank, b):
+                for kp in range(PASSES):
+                    n0 = kp * T * R + a * R + rows_of(i) + rt * P
+                    nc.tensor.matmul_mx(
+                        out=bank[:],
+                        lhsT=h_words[i % R_UNITS, a][:, kp, rt * P : (rt + 1) * P].bitcast(E5M2X4),
+                        lhsT_scale=h_scales[:, n0 : n0 + P],
+                        rhs=b_codes[jg, kp][:].bitcast(E4M3X4),
+                        rhs_scale=b_scales[jg, kp][:],
+                        start=(kp == 0),
+                        stop=(kp == PASSES - 1),
+                    )
+                mx_bank[i, a, k] = (bank, b)
+                busy[b] = True
+
+            return (ready, emit)
+
+        def turn_y(i, jl):
+            def ready():
+                return (i, jl) in y_bf
+
+            def emit(bank, b):
+                words = y_bf[i, jl][:].bitcast(F32)
+                for rt in range(2):
+                    for u in range(2):
+                        nc.tensor.transpose(
+                            bank[:, (2 * u + rt) * P : (2 * u + rt + 1) * P],
+                            words[:, (2 * rt + u) * P : (2 * rt + u + 1) * P],
+                            ident[:],
+                        )
+                y_grouped[i, jl] = ring.tile([P, 4 * UNIT_R], BF16, name="y_grouped", bufs=4, align_bytes=64)
+                nc.scalar.copy(
+                    out=y_grouped[i, jl][:].bitcast(F32).rearrange("p (r u) -> p r u", u=2),
+                    in_=bank[:].rearrange("p (u r) -> p r u", u=2),
+                )
+
+            return (ready, emit)
+
+        for c in range(4):
+            for kp in range(PASSES):
+                stream.append(turn_blocks(c, kp))
+        stream.extend(multiply(0, 0, k) for k in range(4))
+        stream.extend(multiply(0, 1, k) for k in range(4))
+        stream.extend(multiply(1, 0, k) for k in range(2))
+        for i in range(UNITS):
+            if i + 1 < UNITS:
+                stream.extend(multiply(i + 1, 0, k) for k in range(2, 4))
+            if i in (1, 2):
+                for kp in range(PASSES):
+                    for c in range(2 * i + 2, 2 * i + 4):
+                        stream.append(turn_blocks(c, kp))
+            if i + 1 < UNITS:
+                stream.extend(multiply(i + 1, 1, k) for k in range(2))
+            if i >= 1:
+                stream.extend(turn_y(i - 1, jl) for jl in range(2))
+            if i + 1 < UNITS:
+                stream.extend(multiply(i + 1, 1, k) for k in range(2, 4))
+            if i + 2 < UNITS:
+                stream.extend(multiply(i + 2, 0, k) for k in range(2))
+        stream.extend(turn_y(UNITS - 1, jl) for jl in range(2))
+
+        def quantize_blocks(jg, kp):
+            codes = keep.tile([P, GROUP], U32, name="b_codes%d%d" % (jg, kp), align_bytes=64)
+            scales = keep.tile([P, GROUP], U8, name="b_scales%d%d" % (jg, kp), align_bytes=64)
+            nc.vector.quantize_mx(out=codes[:].bitcast(E4M3X4), scales=scales[:], in_=b_grouped[jg, kp][:])
+            b_codes[jg, kp] = codes
+            b_scales[jg, kp] = scales
+            pump()
+
+        def product(i, a, k):
+            if k == 0:
+                prod[i, a] = ring.tile([P, UNIT], F32, name="prod%d" % a, bufs=2)
+            rt, jl = k % 2, k // 2
+            c0 = rt * UNIT_J + jl * GROUP
+            bank, b = mx_bank[i, a, k]
+            nc.vector.tensor_tensor(
+                out=prod[i, a][:, c0 : c0 + GROUP], in0=bank[:], in1=slope_sb[i, a][:, c0 : c0 + GROUP], op=MULT
+            )
+            busy[b] = False
+            pump()
+
+        def add_run(engine, i, cols):
+            engine.tensor_tensor(out=part[i][:, cols], in0=prod[i, 0][:, cols], in1=run_sb[i][:, cols], op=ADD)
+
+        def half_view(tile, jl):
+            return tile[:].rearrange("p (t j) -> p t j", t=2)[:, :, jl * GROUP : (jl + 1) * GROUP]
+
+        def round_y(i, jl):
+            y_bf[i, jl] = ring.tile([P, 2 * GROUP], BF16, name="y_bf", bufs=3, align_bytes=64)
+            nc.scalar.copy(
+                out=y_bf[i, jl][:].rearrange("q (t u p e) -> q t u p e", t=2, u=2, e=2),
+                in_=half_view(y_sb[i], jl).rearrange("q t (p u e) -> q t u p e", u=2, e=2),
+            )
+
+        def quantize_y(i, jl):
+            h = i // R_UNITS
+            r0 = rows_of(i)
+            c0 = r0 - rows_of(first_unit[i])
+            nc.vector.quantize_mx(
+                out=y_codes[first_unit[i]][:, jl, c0 : c0 + UNIT_R].bitcast(E4M3X4),
+                scales=y_scales[h][:, jl, r0 : r0 + UNIT_R],
+                in_=y_grouped[i, jl][:],
+            )
+            pump()
+
+        def store_words(queue, i0):
+            tile = y_codes[i0]
+            h, m0 = i0 // R_UNITS, rows_of(i0)
+            queue.dma_start(
+                out=out_1[2 * h : 2 * h + 2].rearrange("g p m t -> p g (m t)")[
+                    :, :, 4 * m0 : 4 * (m0 + tile.shape[2])
+                ].bitcast(I32),
+                in_=tile[:].bitcast(I32),
+            )
+
+        def store_scales(queue, h, q):
+            queue.dma_start(
+                out=out_2[2 * h : 2 * h + 2, 4 * q : 4 * q + 4, :].rearrange("g r m -> r g m").bitcast(I32),
+                in_=y_scales[h][32 * q : 32 * q + 4, :, :].bitcast(I32),
+            )
+
+        for c in range(4):
+            load_blocks(c)
+        load_h_scales()
+        load_first(0)
+        load_second(0)
+        load_first(1)
+        load_second(1)
+        load_first(2)
+        for c in range(4):
+            sort_blocks(c)
+        for jg in range(2):
+            for kp in range(PASSES):
+                quantize_blocks(jg, kp)
+        load_blocks(4)
+        load_blocks(5)
+        load_second(2)
+        load_first(3)
+        load_blocks(6)
+        load_blocks(7)
+        load_second(3)
+        load_first(4)
+        for k in range(4):
+            product(0, 0, k)
+
+        for i in range(UNITS):
+            last = i == UNITS - 1
+            split = POOL_COLS_LAST if last else POOL_COLS
+            part[i] = ring.tile([P, UNIT], F32, name="part", bufs=1)
+            add_run(nc.gpsimd, i, slice(0, split))
+            for k in range(4):
+                product(i, 1, k)
+            if not last:
+                for k in range(4):
+                    product(i + 1, 0, k)
+            add_run(nc.vector, i, slice(split, UNIT))
+            if i >= 2:
+                for jl in range(2):
+                    quantize_y(i - 2, jl)
+            if i == 2:
+                for jg in (2, 3):
+                    for kp in range(PASSES):
+                        quantize_blocks(jg, kp)
+            y_sb[i] = ring.tile([P, UNIT], F32, name="y", tag="y", bufs=4)
+            if not last:
+                nc.vector.tensor_tensor(out=y_sb[i][:], in0=part[i][:], in1=prod[i, 1][:], op=ADD)
+                for jl in range(2):
+                    round_y(i, jl)
+                if i + 4 < UNITS:
+                    load_second(i + 4)
+                if i + 5 < UNITS:
+                    load_first(i + 5)
+                nc.sync.dma_start(out=unit_view(out_0, i), in_=y_sb[i][:].rearrange("p (t j) -> p t j", t=2))
+                if i == R_UNITS + 1:
+                    store_words(nc.sync, 0)
+                    for q in range(4):
+                        store_scales(nc.sync, 0, q)
+                pump()
+            else:
+                store_words(nc.sync, 4)
+
+                def finish(jl):
+                    nc.vector.tensor_tensor(
+                        out=half_view(y_sb[i], jl), in0=half_view(part[i], jl), in1=half_view(prod[i, 1], jl), op=ADD
+                    )
+                    nc.sync.dma_start(
+                        out=unit_view(out_0, i)[:, :, jl * GROUP : (jl + 1) * GROUP], in_=half_view(y_sb[i], jl)
+                    )
+
+                finish(0)
+                round_y(i, 0)
+                pump()
+                direct = ring.tile([P, 2 * GROUP], BF16, name="y_bf", bufs=3, align_bytes=64)
+                for rt in range(2):
+                    nc.vector.tensor_tensor(
+                        out=direct[:, rt * GROUP : (rt + 1) * GROUP].rearrange("q (u p e) -> q u p e", u=2, e=2),
+                        in0=half_view(part[i], 1)[:, rt, :].rearrange("q (p u e) -> q u p e", u=2, e=2),
+                        in1=half_view(prod[i, 1], 1)[:, rt, :].rearrange("q (p u e) -> q u p e", u=2, e=2),
+                        op=ADD,
+                    )
+                y_bf[i, 1] = direct
+                pump()
+                finish(1)
+                for jl in range(2):
+                    quantize_y(i - 1, jl)
+                store_words(nc.sync, 6)
+                for jl in range(2):
+                    quantize_y(i, jl)
+                store_words(nc.sync, 7)
+                for q in range(4):
+                    store_scales(nc.scalar if q % 2 else nc.sync, 1, q)

@@ -19,15 +19,25 @@ MULT = mybir.AluOpType.mult
 P = 128
 GROUP = 512
 PASSES = NB // GROUP
+BANKS = 8
 CHUNK = 256
-UNIT_R = 256
-UNIT_J = 1024
-UNIT = 2048
+UNIT_R, UNIT_J = 256, 1024
+UNIT = 2 * UNIT_J
 R_UNITS = R // UNIT_R
 UNITS = R_UNITS * (J // UNIT_J)
-BANKS = 8
-POOL_COLS = 1792
+LAST = UNITS - 1
+HEAD_CHUNKS = UNIT_J // CHUNK
+PIECES = range(4)
+
+POOL_COLS = 1856
 POOL_COLS_LAST = 832
+
+TENSOR_SUM_UNITS = [i for i in range(3, UNITS) if i % 2 == 1 or i >= LAST - 1]
+
+QUANTIZE_LAG = 2
+
+CODES_FROM = [0 if i < R_UNITS else i for i in range(UNITS)]
+SCALES_FROM = [0 if i < R_UNITS else i - i % 2 for i in range(UNITS)]
 
 
 def tile_kernel_bin_similarity_gradient_k2_kernel(
@@ -36,143 +46,157 @@ def tile_kernel_bin_similarity_gradient_k2_kernel(
     nc = tc.nc
     with ExitStack() as ctx:
         keep = ctx.enter_context(tc.tile_pool(name="keep", bufs=1))
-        ring = ctx.enter_context(tc.tile_pool(name="ring", bufs=2))
+        ring = ctx.enter_context(tc.tile_pool(name="ring", bufs=1))
         psum = ctx.enter_context(tc.psum_pool(name="psum", bufs=1))
         ctx.enter_context(tc.manual_schedule())
 
         ident = keep.tile([P, P], F32, name="ident")
         make_identity(nc, ident[:])
+
         h_scales = keep.tile([P, PASSES * T * R], U8, name="h_scales", align_bytes=64)
         nc.vector.memset(h_scales[:].bitcast(U32), 0)
 
-        h_words = {}
-        raw = {}
-        sorted_words = {}
-        slope_sb = {}
-        run_sb = {}
-        b_grouped = {}
-        b_codes = {}
-        b_scales = {}
-        prod = {}
-        part = {}
-        y_sb = {}
-        y_bf = {}
-        y_grouped = {}
-        mx_bank = {}
-
-        y_codes = {}
-        first_unit = [0, 0, 0, 0, 4, 4, 6, 7]
-        for i0 in sorted(set(first_unit)):
-            width = first_unit.count(i0) * UNIT_R
+        y_codes, y_scales = {}, {}
+        for i0 in sorted(set(CODES_FROM)):
+            width = CODES_FROM.count(i0) * UNIT_R
             y_codes[i0] = keep.tile([P, 2, width], U32, name="y_codes%d" % i0, align_bytes=64)
-        y_scales = [keep.tile([P, 2, R], U8, name="y_scales%d" % h, align_bytes=64) for h in range(2)]
+        for i0 in sorted(set(SCALES_FROM)):
+            width = SCALES_FROM.count(i0) * UNIT_R
+            y_scales[i0] = keep.tile([P, 2, width], U8, name="y_scales%d" % i0, align_bytes=64)
 
-        def rows_of(i):
+        h_words, slope_sb, run_sb = {}, {}, {}
+        b_raw, b_sorted, b_grouped, b_codes, b_scales = {}, {}, {}, {}, {}
+        mx_bank, prod, part, y_sb = {}, {}, {}, {}
+        y_pairs, y_grouped, run_wide, y_turned = {}, {}, {}, {}
+        multiplied = set()
+
+        def row0(i):
             return (i % R_UNITS) * UNIT_R
 
-        def cols_of(i):
+        def col0(i):
             return (i // R_UNITS) * UNIT_J
 
         def unit_view(dram, i):
-            r0, j0 = rows_of(i), cols_of(i)
-            return dram[r0 : r0 + UNIT_R, j0 : j0 + UNIT_J].rearrange("(t p) j -> p t j", p=P)
+            rows, cols = slice(row0(i), row0(i) + UNIT_R), slice(col0(i), col0(i) + UNIT_J)
+            return dram[rows, cols].rearrange("(rt p) j -> p rt j", p=P)
+
+        def by_row_tile(unit_tile):
+            return unit_tile[:].rearrange("p (rt j) -> p rt j", rt=2)
+
+        def group_view(unit_tile, jl):
+            return by_row_tile(unit_tile)[:, :, jl * GROUP : (jl + 1) * GROUP]
+
+        def row_tiles(i, jl):
+            return range(1 if i in TENSOR_SUM_UNITS and jl == 0 else 0, 2)
+
+        def big_tile(shape, dtype):
+            return ring.tile(shape, dtype, name="big", bufs=4)
+
+        def small_tile(shape, dtype):
+            return ring.tile(shape, dtype, name="small", bufs=4, align_bytes=64)
+
+        def y_tile(i):
+            if i not in y_sb:
+                y_sb[i] = big_tile([P, UNIT], F32)
+            return y_sb[i]
+
+        def y_grouped_tile(i, jl):
+            if (i, jl) not in y_grouped:
+                bufs = 2 * (QUANTIZE_LAG + 1)
+                y_grouped[i, jl] = ring.tile([P, 4 * UNIT_R], BF16, name="y_grouped", bufs=bufs, align_bytes=64)
+            return y_grouped[i, jl]
+
+        def y_pairs_tile(i, jl):
+            y_pairs[i, jl] = ring.tile([P, 2 * GROUP], BF16, name="y_pairs", bufs=3, align_bytes=64)
+            return y_pairs[i, jl]
+
 
         def load_blocks(c):
-            raw[c] = ring.tile([P, 2 * NB], BF16, name="raw", bufs=4, align_bytes=64)
-            nc.sync.dma_start(
-                out=raw[c][:],
-                in_=blocks[c * CHUNK : (c + 1) * CHUNK, :].rearrange("(p s) k -> p (s k)", s=2),
-            )
+            b_raw[c] = ring.tile([P, 2 * NB], BF16, name="b_raw", bufs=HEAD_CHUNKS, align_bytes=64)
+            rows = blocks[c * CHUNK : (c + 1) * CHUNK, :]
+            nc.sync.dma_start(out=b_raw[c][:], in_=rows.rearrange("(p s) b -> p (s b)", s=2))
 
         def load_h_scales():
             for q in range(4):
                 nc.sync.dma_start(
-                    out=h_scales[32 * q : 32 * q + 4, :].bitcast(I32).rearrange("r (g n) -> r g n", g=PASSES),
-                    in_=g_scales[:, 4 * q : 4 * q + 4, :].rearrange("g r n -> r g n").bitcast(I32),
+                    out=h_scales[32 * q : 32 * q + 4, :].bitcast(I32).rearrange("s (g n) -> s g n", g=PASSES),
+                    in_=g_scales[:, 4 * q : 4 * q + 4, :].rearrange("g s n -> s g n").bitcast(I32),
                 )
 
-        def load_h_words(i, a):
-            h_words[i, a] = keep.tile([P, PASSES, UNIT_R], U32, name="h_words%d%d" % (i, a), align_bytes=64)
-            n0 = a * R + rows_of(i)
-            nc.sync.dma_start(
-                out=h_words[i, a][:].bitcast(I32),
-                in_=g_words.rearrange("g p n t -> p g (n t)")[:, :, 4 * n0 : 4 * (n0 + UNIT_R)].bitcast(I32),
-            )
-
-        def load_slope(i, a):
+        def load_bin(i, a):
+            if i < R_UNITS:
+                h_words[i, a] = keep.tile([P, PASSES, UNIT_R], U32, name="h_words%d%d" % (i, a), align_bytes=64)
+                n0 = a * R + row0(i)
+                nc.sync.dma_start(
+                    out=h_words[i, a][:].bitcast(I32),
+                    in_=g_words.rearrange("g p n t -> p g (n t)")[:, :, 4 * n0 : 4 * (n0 + UNIT_R)].bitcast(I32),
+                )
             slope_sb[i, a] = ring.tile([P, UNIT], BF16, name="slope%d" % a, bufs=5 - a)
-            nc.sync.dma_start(out=slope_sb[i, a][:].rearrange("p (t j) -> p t j", t=2), in_=unit_view(slope[a], i))
+            nc.sync.dma_start(out=by_row_tile(slope_sb[i, a]), in_=unit_view(slope[a], i))
 
-        def load_run(i):
+        def load_bin_1_and_run(i):
+            load_bin(i, 1)
             run_sb[i] = ring.tile([P, UNIT], BF16, name="run", bufs=4)
-            nc.sync.dma_start(out=run_sb[i][:].rearrange("p (t j) -> p t j", t=2), in_=unit_view(run, i))
+            nc.sync.dma_start(out=by_row_tile(run_sb[i]), in_=unit_view(run, i))
 
-        def load_first(i):
-            if i < R_UNITS:
-                load_h_words(i, 0)
-            load_slope(i, 0)
+        def store_planes(i):
+            g0 = col0(i) // GROUP
+            if i == LAST or CODES_FROM[i + 1] != CODES_FROM[i]:
+                codes, m0 = y_codes[CODES_FROM[i]], row0(CODES_FROM[i])
+                dram = out_1[g0 : g0 + 2].rearrange("g p m t -> p g (m t)")
+                nc.sync.dma_start(
+                    out=dram[:, :, 4 * m0 : 4 * (m0 + codes.shape[2])].bitcast(I32), in_=codes[:].bitcast(I32)
+                )
+            if i == LAST or SCALES_FROM[i + 1] != SCALES_FROM[i]:
+                scales, m0 = y_scales[SCALES_FROM[i]], row0(SCALES_FROM[i])
+                for q in range(4):
+                    queue = nc.scalar if i == LAST and q % 2 else nc.sync
+                    dram = out_2[g0 : g0 + 2, 4 * q : 4 * q + 4, m0 : m0 + scales.shape[2]]
+                    queue.dma_start(
+                        out=dram.rearrange("g s m -> s g m").bitcast(I32),
+                        in_=scales[32 * q : 32 * q + 4, :, :].bitcast(I32),
+                    )
 
-        def load_second(i):
-            if i < R_UNITS:
-                load_h_words(i, 1)
-            load_slope(i, 1)
-            load_run(i)
 
-        stream = []
-        busy = [False] * BANKS
-        issued = [0]
+        jobs = []
+        taken = [False] * BANKS
+        written = [0]
 
-        def pump():
-            while issued[0] < len(stream):
-                item = stream[issued[0]]
-                b = issued[0] % BANKS
-                if busy[b] or not item[0]():
+        def write_jobs():
+            while written[0] < len(jobs):
+                ready, write = jobs[written[0]]
+                b = written[0] % BANKS
+                if taken[b] or not ready():
                     break
-                bank = psum.tile([P, GROUP], F32, name="bank%d" % b)
-                issued[0] = issued[0] + 1
-                item[1](bank, b)
-
-        def sort_blocks(c):
-            sorted_words[c] = ring.tile([P, NB], F32, name="sorted_words", tag="y", bufs=4)
-            nc.vector.tensor_copy(
-                out=sorted_words[c][:].rearrange("p (x u w) -> p x u w", x=4, u=2),
-                in_=raw[c][:].bitcast(F32).rearrange("p (x w u) -> p x u w", x=4, u=2),
-            )
-            pump()
+                written[0] = written[0] + 1
+                write(psum.tile([P, GROUP], F32, name="bank%d" % b), b)
 
         def turn_blocks(c, kp):
-            def ready():
-                return c in (sorted_words if c < 4 else raw)
-
-            def emit(bank, b):
+            def write(bank, b):
                 for s in range(2):
                     for u in range(2):
-                        w0 = s * (NB // 2) + kp * 256
-                        if c < 4:
-                            words = sorted_words[c][:, w0 + u * P : w0 + (u + 1) * P]
+                        w0 = s * (NB // 2) + kp * (GROUP // 2)
+                        if c < HEAD_CHUNKS:
+                            pairs = b_sorted[c][:, w0 + u * P : w0 + (u + 1) * P]
                         else:
-                            words = raw[c][:].bitcast(F32)[:, w0 + u : w0 + 256 : 2]
-                        nc.tensor.transpose(bank[:, (2 * s + u) * P : (2 * s + u + 1) * P], words, ident[:])
+                            pairs = b_raw[c][:].bitcast(F32)[:, w0 + u : w0 + GROUP // 2 : 2]
+                        nc.tensor.transpose(bank[:, (2 * s + u) * P : (2 * s + u + 1) * P], pairs, ident[:])
                 key = (c // 2, kp)
                 if key not in b_grouped:
-                    b_grouped[key] = ring.tile([P, 4 * GROUP], BF16, name="b_grouped", bufs=4, align_bytes=64)
-                dst = b_grouped[key][:].bitcast(F32)[:, (c % 2) * GROUP : (c % 2 + 1) * GROUP]
-                dst = dst.rearrange("q (p x) -> q p x", x=4)
-                src = bank[:].rearrange("q (x p) -> q p x", x=4)
-                nc.scalar.copy(out=dst, in_=src)
+                    b_grouped[key] = small_tile([P, 4 * GROUP], BF16)
+                half = b_grouped[key][:].bitcast(F32)[:, (c % 2) * GROUP : (c % 2 + 1) * GROUP]
+                nc.scalar.copy(
+                    out=half.rearrange("p (m su) -> p m su", su=4), in_=bank[:].rearrange("p (su m) -> p m su", su=4)
+                )
 
-            return (ready, emit)
+            return (lambda: c in (b_sorted if c < HEAD_CHUNKS else b_raw), write)
 
         def multiply(i, a, k):
-            rt, jl = k % 2, k // 2
-            jg = cols_of(i) // GROUP + jl
+            rt, jg = k % 2, col0(i) // GROUP + k // 2
 
-            def ready():
-                return all((jg, kp) in b_codes for kp in range(PASSES)) and (i % R_UNITS, a) in h_words
-
-            def emit(bank, b):
+            def write(bank, b):
                 for kp in range(PASSES):
-                    n0 = kp * T * R + a * R + rows_of(i) + rt * P
+                    n0 = kp * T * R + a * R + row0(i) + rt * P
                     nc.tensor.matmul_mx(
                         out=bank[:],
                         lhsT=h_words[i % R_UNITS, a][:, kp, rt * P : (rt + 1) * P].bitcast(E5M2X4),
@@ -183,201 +207,223 @@ def tile_kernel_bin_similarity_gradient_k2_kernel(
                         stop=(kp == PASSES - 1),
                     )
                 mx_bank[i, a, k] = (bank, b)
-                busy[b] = True
+                taken[b] = True
 
-            return (ready, emit)
+            return (lambda: (jg, PASSES - 1) in b_codes, write)
 
         def turn_y(i, jl):
-            def ready():
-                return (i, jl) in y_bf
-
-            def emit(bank, b):
-                words = y_bf[i, jl][:].bitcast(F32)
-                for rt in range(2):
+            def write(bank, b):
+                pairs = y_pairs[i, jl][:].bitcast(F32)
+                for rt in row_tiles(i, jl):
                     for u in range(2):
                         nc.tensor.transpose(
                             bank[:, (2 * u + rt) * P : (2 * u + rt + 1) * P],
-                            words[:, (2 * rt + u) * P : (2 * rt + u + 1) * P],
+                            pairs[:, (2 * rt + u) * P : (2 * rt + u + 1) * P],
                             ident[:],
                         )
-                y_grouped[i, jl] = ring.tile([P, 4 * UNIT_R], BF16, name="y_grouped", bufs=4, align_bytes=64)
+                rows = slice(row_tiles(i, jl).start * P, UNIT_R)
                 nc.scalar.copy(
-                    out=y_grouped[i, jl][:].bitcast(F32).rearrange("p (r u) -> p r u", u=2),
-                    in_=bank[:].rearrange("p (u r) -> p r u", u=2),
+                    out=y_grouped_tile(i, jl)[:].bitcast(F32).rearrange("p (r u) -> p r u", u=2)[:, rows, :],
+                    in_=bank[:].rearrange("p (u r) -> p r u", u=2)[:, rows, :],
                 )
 
-            return (ready, emit)
+            return (lambda: (i, jl) in y_pairs, write)
 
-        for c in range(4):
-            for kp in range(PASSES):
-                stream.append(turn_blocks(c, kp))
-        stream.extend(multiply(0, 0, k) for k in range(4))
-        stream.extend(multiply(0, 1, k) for k in range(4))
-        stream.extend(multiply(1, 0, k) for k in range(2))
+        def sum_on_tensor(i):
+            def write(bank, b):
+                terms = (run_wide[i], prod[i, 0], prod[i, 1])
+                for t in range(4):
+                    cols = slice(t * P, (t + 1) * P)
+                    for n, term in enumerate(terms):
+                        first, final = n == 0, n == len(terms) - 1
+                        nc.tensor.matmul(
+                            bank[:, cols], term[:, cols], ident[:], start=first, stop=final, is_transpose=True
+                        )
+                y_turned[i] = small_tile([P, GROUP], F32)
+                nc.scalar.copy(out=y_turned[i][:], in_=bank[:])
+                nc.scalar.copy(
+                    out=y_grouped_tile(i, 0)[:, 0 : 4 * P].rearrange("p (r t) -> p r t", t=4),
+                    in_=bank[:].rearrange("p (t r) -> p r t", t=4),
+                )
+
+            return (lambda: (i, 1, 0) in multiplied, write)
+
+        def turn_back(i):
+            def write(bank, b):
+                for t in range(4):
+                    cols = slice(t * P, (t + 1) * P)
+                    nc.tensor.transpose(bank[:, cols], y_turned[i][:, cols], ident[:])
+                nc.scalar.copy(
+                    out=y_tile(i)[:, 0:GROUP].rearrange("r (p t) -> r p t", t=4),
+                    in_=bank[:].rearrange("r (t p) -> r p t", t=4),
+                )
+
+            return (lambda: i in y_turned, write)
+
+        late_chunks = {place + 1: c for place, c in enumerate(range(HEAD_CHUNKS, J // CHUNK))}
+        for c in range(HEAD_CHUNKS):
+            jobs.extend(turn_blocks(c, kp) for kp in range(PASSES))
+        jobs.extend(multiply(0, 0, k) for k in PIECES)
+        jobs.extend(multiply(0, 1, k) for k in PIECES)
+        jobs.extend(multiply(1, 0, k) for k in PIECES[:2])
         for i in range(UNITS):
-            if i + 1 < UNITS:
-                stream.extend(multiply(i + 1, 0, k) for k in range(2, 4))
-            if i in (1, 2):
-                for kp in range(PASSES):
-                    for c in range(2 * i + 2, 2 * i + 4):
-                        stream.append(turn_blocks(c, kp))
-            if i + 1 < UNITS:
-                stream.extend(multiply(i + 1, 1, k) for k in range(2))
-            if i >= 1:
-                stream.extend(turn_y(i - 1, jl) for jl in range(2))
-            if i + 1 < UNITS:
-                stream.extend(multiply(i + 1, 1, k) for k in range(2, 4))
-            if i + 2 < UNITS:
-                stream.extend(multiply(i + 2, 0, k) for k in range(2))
-        stream.extend(turn_y(UNITS - 1, jl) for jl in range(2))
+            if i < LAST:
+                jobs.extend(multiply(i + 1, 0, k) for k in PIECES[2:])
+            if 2 * i in late_chunks:
+                jobs.extend(turn_blocks(late_chunks[2 * i], kp) for kp in range(PASSES))
+            if i in TENSOR_SUM_UNITS:
+                jobs.append(sum_on_tensor(i))
+            if i < LAST:
+                jobs.extend(multiply(i + 1, 1, k) for k in PIECES[:2])
+            if i > 0:
+                jobs.extend(turn_y(i - 1, jl) for jl in range(2))
+            if 2 * i + 1 in late_chunks:
+                jobs.extend(turn_blocks(late_chunks[2 * i + 1], kp) for kp in range(PASSES))
+            if i in TENSOR_SUM_UNITS:
+                jobs.append(turn_back(i))
+            if i < LAST:
+                jobs.extend(multiply(i + 1, 1, k) for k in PIECES[2:])
+            if i + 1 < LAST:
+                jobs.extend(multiply(i + 2, 0, k) for k in PIECES[:2])
+        jobs.extend(turn_y(LAST, jl) for jl in (1, 0))
 
-        def quantize_blocks(jg, kp):
-            codes = keep.tile([P, GROUP], U32, name="b_codes%d%d" % (jg, kp), align_bytes=64)
-            scales = keep.tile([P, GROUP], U8, name="b_scales%d%d" % (jg, kp), align_bytes=64)
-            nc.vector.quantize_mx(out=codes[:].bitcast(E4M3X4), scales=scales[:], in_=b_grouped[jg, kp][:])
-            b_codes[jg, kp] = codes
-            b_scales[jg, kp] = scales
-            pump()
+
+        def sort_blocks(c):
+            b_sorted[c] = big_tile([P, NB], F32)
+            for kp in range(PASSES):
+                nc.vector.tensor_copy(
+                    out=b_sorted[c][:].rearrange("m (s g u p) -> m g s u p", s=2, g=PASSES, u=2)[:, kp],
+                    in_=b_raw[c][:].bitcast(F32).rearrange("m (s g p u) -> m g s u p", s=2, g=PASSES, u=2)[:, kp],
+                )
+            write_jobs()
+
+        def quantize_blocks(jg):
+            for kp in range(PASSES):
+                codes = keep.tile([P, GROUP], U32, name="b_codes%d%d" % (jg, kp), align_bytes=64)
+                scales = keep.tile([P, GROUP], U8, name="b_scales%d%d" % (jg, kp), align_bytes=64)
+                nc.vector.quantize_mx(out=codes[:].bitcast(E4M3X4), scales=scales[:], in_=b_grouped[jg, kp][:])
+                b_codes[jg, kp], b_scales[jg, kp] = codes, scales
+            write_jobs()
 
         def product(i, a, k):
             if k == 0:
                 prod[i, a] = ring.tile([P, UNIT], F32, name="prod%d" % a, bufs=2)
-            rt, jl = k % 2, k // 2
-            c0 = rt * UNIT_J + jl * GROUP
+            c0 = (k % 2) * UNIT_J + (k // 2) * GROUP
             bank, b = mx_bank[i, a, k]
-            nc.vector.tensor_tensor(
-                out=prod[i, a][:, c0 : c0 + GROUP], in0=bank[:], in1=slope_sb[i, a][:, c0 : c0 + GROUP], op=MULT
+            dst, src, factor = prod[i, a][:, c0 : c0 + GROUP], bank[:], slope_sb[i, a][:, c0 : c0 + GROUP]
+            if i in TENSOR_SUM_UNITS and k == 0:
+                dst = dst.rearrange("r (t p) -> r t p", t=4)
+                src = src.rearrange("r (p t) -> r t p", t=4)
+                factor = factor.rearrange("r (p t) -> r t p", t=4)
+            nc.vector.tensor_tensor(out=dst, in0=src, in1=factor, op=MULT)
+            multiplied.add((i, a, k))
+            taken[b] = False
+            write_jobs()
+
+        def widen_run(i):
+            run_wide[i] = small_tile([P, GROUP], F32)
+            nc.scalar.copy(
+                out=run_wide[i][:].rearrange("r (t p) -> r t p", t=4),
+                in_=run_sb[i][:, 0:GROUP].rearrange("r (p t) -> r t p", t=4),
             )
-            busy[b] = False
-            pump()
 
         def add_run(engine, i, cols):
             engine.tensor_tensor(out=part[i][:, cols], in0=prod[i, 0][:, cols], in1=run_sb[i][:, cols], op=ADD)
 
-        def half_view(tile, jl):
-            return tile[:].rearrange("p (t j) -> p t j", t=2)[:, :, jl * GROUP : (jl + 1) * GROUP]
+        def add_bin_1(i, cols):
+            nc.vector.tensor_tensor(out=y_tile(i)[:, cols], in0=part[i][:, cols], in1=prod[i, 1][:, cols], op=ADD)
 
         def round_y(i, jl):
-            y_bf[i, jl] = ring.tile([P, 2 * GROUP], BF16, name="y_bf", bufs=3, align_bytes=64)
+            rts = slice(row_tiles(i, jl).start, 2)
             nc.scalar.copy(
-                out=y_bf[i, jl][:].rearrange("q (t u p e) -> q t u p e", t=2, u=2, e=2),
-                in_=half_view(y_sb[i], jl).rearrange("q t (p u e) -> q t u p e", u=2, e=2),
+                out=y_pairs_tile(i, jl)[:].rearrange("r (rt u p e) -> r rt u p e", rt=2, u=2, e=2)[:, rts],
+                in_=group_view(y_sb[i], jl).rearrange("r rt (p u e) -> r rt u p e", u=2, e=2)[:, rts],
             )
+
+        def add_bin_1_rounded(i, jl):
+            pairs = y_pairs_tile(i, jl)
+            for rt in range(2):
+                nc.vector.tensor_tensor(
+                    out=pairs[:, rt * GROUP : (rt + 1) * GROUP].rearrange("r (u p e) -> r u p e", u=2, e=2),
+                    in0=group_view(part[i], jl)[:, rt, :].rearrange("r (p u e) -> r u p e", u=2, e=2),
+                    in1=group_view(prod[i, 1], jl)[:, rt, :].rearrange("r (p u e) -> r u p e", u=2, e=2),
+                    op=ADD,
+                )
+            write_jobs()
 
         def quantize_y(i, jl):
-            h = i // R_UNITS
-            r0 = rows_of(i)
-            c0 = r0 - rows_of(first_unit[i])
+            c0, s0 = row0(i) - row0(CODES_FROM[i]), row0(i) - row0(SCALES_FROM[i])
             nc.vector.quantize_mx(
-                out=y_codes[first_unit[i]][:, jl, c0 : c0 + UNIT_R].bitcast(E4M3X4),
-                scales=y_scales[h][:, jl, r0 : r0 + UNIT_R],
+                out=y_codes[CODES_FROM[i]][:, jl, c0 : c0 + UNIT_R].bitcast(E4M3X4),
+                scales=y_scales[SCALES_FROM[i]][:, jl, s0 : s0 + UNIT_R],
                 in_=y_grouped[i, jl][:],
             )
-            pump()
+            write_jobs()
 
-        def store_words(queue, i0):
-            tile = y_codes[i0]
-            h, m0 = i0 // R_UNITS, rows_of(i0)
-            queue.dma_start(
-                out=out_1[2 * h : 2 * h + 2].rearrange("g p m t -> p g (m t)")[
-                    :, :, 4 * m0 : 4 * (m0 + tile.shape[2])
-                ].bitcast(I32),
-                in_=tile[:].bitcast(I32),
-            )
 
-        def store_scales(queue, h, q):
-            queue.dma_start(
-                out=out_2[2 * h : 2 * h + 2, 4 * q : 4 * q + 4, :].rearrange("g r m -> r g m").bitcast(I32),
-                in_=y_scales[h][32 * q : 32 * q + 4, :, :].bitcast(I32),
-            )
-
-        for c in range(4):
+        for c in range(HEAD_CHUNKS):
             load_blocks(c)
         load_h_scales()
-        load_first(0)
-        load_second(0)
-        load_first(1)
-        load_second(1)
-        load_first(2)
-        for c in range(4):
+        for c in range(HEAD_CHUNKS):
             sort_blocks(c)
-        for jg in range(2):
-            for kp in range(PASSES):
-                quantize_blocks(jg, kp)
-        load_blocks(4)
-        load_blocks(5)
-        load_second(2)
-        load_first(3)
-        load_blocks(6)
-        load_blocks(7)
-        load_second(3)
-        load_first(4)
-        for k in range(4):
+        load_bin(0, 0)
+        load_bin_1_and_run(0)
+        for place in range(1, 2 * R_UNITS):
+            if place % 2 == 1:
+                load_bin((place + 1) // 2, 0)
+            else:
+                load_bin_1_and_run(place // 2)
+            if place in late_chunks:
+                load_blocks(late_chunks[place])
+        for jg in range(UNIT_J // GROUP):
+            quantize_blocks(jg)
+        for k in PIECES:
             product(0, 0, k)
 
+
         for i in range(UNITS):
-            last = i == UNITS - 1
-            split = POOL_COLS_LAST if last else POOL_COLS
+            first = GROUP if i in TENSOR_SUM_UNITS else 0
+            split = min(UNIT, first + (POOL_COLS_LAST if i == LAST else POOL_COLS))
             part[i] = ring.tile([P, UNIT], F32, name="part", bufs=1)
-            add_run(nc.gpsimd, i, slice(0, split))
-            for k in range(4):
+            add_run(nc.gpsimd, i, slice(first, split))
+            for k in PIECES:
                 product(i, 1, k)
-            if not last:
-                for k in range(4):
+            if i + 1 in TENSOR_SUM_UNITS:
+                widen_run(i + 1)
+            if i < LAST:
+                for k in PIECES:
                     product(i + 1, 0, k)
-            add_run(nc.vector, i, slice(split, UNIT))
-            if i >= 2:
+            if split < UNIT:
+                add_run(nc.vector, i, slice(split, UNIT))
+            if i >= QUANTIZE_LAG:
                 for jl in range(2):
-                    quantize_y(i - 2, jl)
-            if i == 2:
-                for jg in (2, 3):
-                    for kp in range(PASSES):
-                        quantize_blocks(jg, kp)
-            y_sb[i] = ring.tile([P, UNIT], F32, name="y", tag="y", bufs=4)
-            if not last:
-                nc.vector.tensor_tensor(out=y_sb[i][:], in0=part[i][:], in1=prod[i, 1][:], op=ADD)
+                    quantize_y(i - QUANTIZE_LAG, jl)
+            if 2 * i in late_chunks:
+                quantize_blocks(late_chunks[2 * i] // 2)
+            if i < LAST:
+                add_bin_1(i, slice(first, UNIT))
                 for jl in range(2):
                     round_y(i, jl)
-                if i + 4 < UNITS:
-                    load_second(i + 4)
-                if i + 5 < UNITS:
-                    load_first(i + 5)
-                nc.sync.dma_start(out=unit_view(out_0, i), in_=y_sb[i][:].rearrange("p (t j) -> p t j", t=2))
-                if i == R_UNITS + 1:
-                    store_words(nc.sync, 0)
-                    for q in range(4):
-                        store_scales(nc.sync, 0, q)
-                pump()
-            else:
-                store_words(nc.sync, 4)
+                if i + R_UNITS < UNITS:
+                    load_bin_1_and_run(i + R_UNITS)
+                if i + R_UNITS + 1 < UNITS:
+                    load_bin(i + R_UNITS + 1, 0)
+            if i >= QUANTIZE_LAG:
+                store_planes(i - QUANTIZE_LAG)
+            if i < LAST:
+                nc.sync.dma_start(out=unit_view(out_0, i), in_=by_row_tile(y_sb[i]))
+                write_jobs()
 
-                def finish(jl):
-                    nc.vector.tensor_tensor(
-                        out=half_view(y_sb[i], jl), in0=half_view(part[i], jl), in1=half_view(prod[i, 1], jl), op=ADD
-                    )
-                    nc.sync.dma_start(
-                        out=unit_view(out_0, i)[:, :, jl * GROUP : (jl + 1) * GROUP], in_=half_view(y_sb[i], jl)
-                    )
 
-                finish(0)
-                round_y(i, 0)
-                pump()
-                direct = ring.tile([P, 2 * GROUP], BF16, name="y_bf", bufs=3, align_bytes=64)
-                for rt in range(2):
-                    nc.vector.tensor_tensor(
-                        out=direct[:, rt * GROUP : (rt + 1) * GROUP].rearrange("q (u p e) -> q u p e", u=2, e=2),
-                        in0=half_view(part[i], 1)[:, rt, :].rearrange("q (p u e) -> q u p e", u=2, e=2),
-                        in1=half_view(prod[i, 1], 1)[:, rt, :].rearrange("q (p u e) -> q u p e", u=2, e=2),
-                        op=ADD,
-                    )
-                y_bf[i, 1] = direct
-                pump()
-                finish(1)
-                for jl in range(2):
-                    quantize_y(i - 1, jl)
-                store_words(nc.sync, 6)
-                for jl in range(2):
-                    quantize_y(i, jl)
-                store_words(nc.sync, 7)
-                for q in range(4):
-                    store_scales(nc.scalar if q % 2 else nc.sync, 1, q)
+        add_bin_1(LAST, slice(UNIT_J, UNIT))
+        round_y(LAST, 0)
+        nc.sync.dma_start(out=unit_view(out_0, LAST)[:, 1, :], in_=y_sb[LAST][:, UNIT_J:UNIT])
+        add_bin_1_rounded(LAST, 1)
+        add_bin_1(LAST, slice(GROUP, UNIT_J))
+        nc.sync.dma_start(out=unit_view(out_0, LAST)[:, 0, :], in_=y_sb[LAST][:, 0:UNIT_J])
+        for jl in range(2):
+            quantize_y(LAST - 1, jl)
+        store_planes(LAST - 1)
+        for jl in (1, 0):
+            quantize_y(LAST, jl)
+        store_planes(LAST)

@@ -117,10 +117,10 @@ def tile_kernel_bin_similarity_gradient_k2_kernel(
             nc.sync.dma_start(out=b_raw[c][:], in_=rows.rearrange("(p s) b -> p (s b)", s=2))
 
         def load_h_scales():
-            for q in range(4):
+            for s in range(4):
                 nc.sync.dma_start(
-                    out=h_scales[32 * q : 32 * q + 4, :].bitcast(I32).rearrange("s (g n) -> s g n", g=PASSES),
-                    in_=g_scales[:, 4 * q : 4 * q + 4, :].rearrange("g s n -> s g n").bitcast(I32),
+                    out=h_scales[s:P:32, :].bitcast(I32).rearrange("q (g n) -> q g n", g=PASSES),
+                    in_=g_scales[:, s:16:4, :].rearrange("g q n -> q g n").bitcast(I32),
                 )
 
         def load_bin(i, a):
@@ -149,12 +149,11 @@ def tile_kernel_bin_similarity_gradient_k2_kernel(
                 )
             if i == LAST or SCALES_FROM[i + 1] != SCALES_FROM[i]:
                 scales, m0 = y_scales[SCALES_FROM[i]], row0(SCALES_FROM[i])
-                for q in range(4):
-                    queue = nc.scalar if i == LAST and q % 2 else nc.sync
-                    dram = out_2[g0 : g0 + 2, 4 * q : 4 * q + 4, m0 : m0 + scales.shape[2]]
+                for s in range(4):
+                    queue = nc.scalar if i == LAST and s % 2 else nc.sync
+                    dram = out_2[g0 : g0 + 2, s:16:4, m0 : m0 + scales.shape[2]]
                     queue.dma_start(
-                        out=dram.rearrange("g s m -> s g m").bitcast(I32),
-                        in_=scales[32 * q : 32 * q + 4, :, :].bitcast(I32),
+                        out=dram.rearrange("g q m -> q g m").bitcast(I32), in_=scales[s:P:32, :, :].bitcast(I32)
                     )
 
 

@@ -32,7 +32,7 @@ PIECES = range(4)
 POOL_COLS = 1856
 POOL_COLS_LAST = 832
 
-TENSOR_SUM_UNITS = [i for i in range(3, UNITS) if i % 2 == 1 or i >= LAST - 1]
+TENSOR_SUM_UNITS = range(3, UNITS)
 
 QUANTIZE_LAG = 2
 

from contextlib import ExitStack

import concourse.mybir as mybir
from concourse.masks import make_identity

T, R, J, NB = 2, 1024, 2048, 1024
FLOPS = 2 * T * R * J * NB

F32 = mybir.dt.float32
BF16 = mybir.dt.bfloat16
U32 = mybir.dt.uint32
I32 = mybir.dt.int32
U8 = mybir.dt.uint8
E4M3X4 = mybir.dt.float8_e4m3fn_x4
E5M2X4 = mybir.dt.float8_e5m2_x4
ADD = mybir.AluOpType.add
MULT = mybir.AluOpType.mult

P = 128
GROUP = 512
PASSES = NB // GROUP
BANKS = 8
CHUNK = 256
UNIT_R, UNIT_J = 256, 1024
UNIT = 2 * UNIT_J
R_UNITS = R // UNIT_R
UNITS = R_UNITS * (J // UNIT_J)
LAST = UNITS - 1
HEAD_CHUNKS = UNIT_J // CHUNK
PIECES = range(4)

POOL_COLS = 1856
POOL_COLS_LAST = 832

TENSOR_SUM_UNITS = range(3, UNITS)

QUANTIZE_LAG = 2

CODES_FROM = [0 if i < R_UNITS else i for i in range(UNITS)]
SCALES_FROM = [0 if i < R_UNITS else i - i % 2 for i in range(UNITS)]


def tile_kernel_bin_similarity_gradient_k2_kernel(
    tc, g_words, g_scales, blocks, slope, run, out_0, out_1, out_2
):
    nc = tc.nc
    with ExitStack() as ctx:
        keep = ctx.enter_context(tc.tile_pool(name="keep", bufs=1))
        ring = ctx.enter_context(tc.tile_pool(name="ring", bufs=1))
        psum = ctx.enter_context(tc.psum_pool(name="psum", bufs=1))
        ctx.enter_context(tc.manual_schedule())

        ident = keep.tile([P, P], F32, name="ident")
        make_identity(nc, ident[:])

        h_scales = keep.tile([P, PASSES * T * R], U8, name="h_scales", align_bytes=64)
        nc.vector.memset(h_scales[:].bitcast(U32), 0)

        y_codes, y_scales = {}, {}
        for i0 in sorted(set(CODES_FROM)):
            width = CODES_FROM.count(i0) * UNIT_R
            y_codes[i0] = keep.tile([P, 2, width], U32, name="y_codes%d" % i0, align_bytes=64)
        for i0 in sorted(set(SCALES_FROM)):
            width = SCALES_FROM.count(i0) * UNIT_R
            y_scales[i0] = keep.tile([P, 2, width], U8, name="y_scales%d" % i0, align_bytes=64)

        h_words, slope_sb, run_sb = {}, {}, {}
        b_raw, b_sorted, b_grouped, b_codes, b_scales = {}, {}, {}, {}, {}
        mx_bank, prod, part, y_sb = {}, {}, {}, {}
        y_pairs, y_grouped, run_wide, y_turned = {}, {}, {}, {}
        multiplied = set()

        def row0(i):
            return (i % R_UNITS) * UNIT_R

        def col0(i):
            return (i // R_UNITS) * UNIT_J

        def unit_view(dram, i):
            rows, cols = slice(row0(i), row0(i) + UNIT_R), slice(col0(i), col0(i) + UNIT_J)
            return dram[rows, cols].rearrange("(rt p) j -> p rt j", p=P)

        def by_row_tile(unit_tile):
            return unit_tile[:].rearrange("p (rt j) -> p rt j", rt=2)

        def group_view(unit_tile, jl):
            return by_row_tile(unit_tile)[:, :, jl * GROUP : (jl + 1) * GROUP]

        def row_tiles(i, jl):
            return range(1 if i in TENSOR_SUM_UNITS and jl == 0 else 0, 2)

        def big_tile(shape, dtype):
            return ring.tile(shape, dtype, name="big", bufs=4)

        def small_tile(shape, dtype):
            return ring.tile(shape, dtype, name="small", bufs=4, align_bytes=64)

        def y_tile(i):
            if i not in y_sb:
                y_sb[i] = big_tile([P, UNIT], F32)
            return y_sb[i]

        def y_grouped_tile(i, jl):
            if (i, jl) not in y_grouped:
                bufs = 2 * (QUANTIZE_LAG + 1)
                y_grouped[i, jl] = ring.tile([P, 4 * UNIT_R], BF16, name="y_grouped", bufs=bufs, align_bytes=64)
            return y_grouped[i, jl]

        def y_pairs_tile(i, jl):
            y_pairs[i, jl] = ring.tile([P, 2 * GROUP], BF16, name="y_pairs", bufs=3, align_bytes=64)
            return y_pairs[i, jl]


        def load_blocks(c):
            b_raw[c] = ring.tile([P, 2 * NB], BF16, name="b_raw", bufs=HEAD_CHUNKS, align_bytes=64)
            rows = blocks[c * CHUNK : (c + 1) * CHUNK, :]
            nc.sync.dma_start(out=b_raw[c][:], in_=rows.rearrange("(p s) b -> p (s b)", s=2))

        def load_h_scales():
            for s in range(4):
                nc.sync.dma_start(
                    out=h_scales[s:P:32, :].bitcast(I32).rearrange("q (g n) -> q g n", g=PASSES),
                    in_=g_scales[:, s:16:4, :].rearrange("g q n -> q g n").bitcast(I32),
                )

        def load_bin(i, a):
            if i < R_UNITS:
                h_words[i, a] = keep.tile([P, PASSES, UNIT_R], U32, name="h_words%d%d" % (i, a), align_bytes=64)
                n0 = a * R + row0(i)
                nc.sync.dma_start(
                    out=h_words[i, a][:].bitcast(I32),
                    in_=g_words.rearrange("g p n t -> p g (n t)")[:, :, 4 * n0 : 4 * (n0 + UNIT_R)].bitcast(I32),
                )
            slope_sb[i, a] = ring.tile([P, UNIT], BF16, name="slope%d" % a, bufs=5 - a)
            nc.sync.dma_start(out=by_row_tile(slope_sb[i, a]), in_=unit_view(slope[a], i))

        def load_bin_1_and_run(i):
            load_bin(i, 1)
            run_sb[i] = ring.tile([P, UNIT], BF16, name="run", bufs=4)
            nc.sync.dma_start(out=by_row_tile(run_sb[i]), in_=unit_view(run, i))

        def store_planes(i):
            g0 = col0(i) // GROUP
            if i == LAST or CODES_FROM[i + 1] != CODES_FROM[i]:
                codes, m0 = y_codes[CODES_FROM[i]], row0(CODES_FROM[i])
                dram = out_1[g0 : g0 + 2].rearrange("g p m t -> p g (m t)")
                nc.sync.dma_start(
                    out=dram[:, :, 4 * m0 : 4 * (m0 + codes.shape[2])].bitcast(I32), in_=codes[:].bitcast(I32)
                )
            if i == LAST or SCALES_FROM[i + 1] != SCALES_FROM[i]:
                scales, m0 = y_scales[SCALES_FROM[i]], row0(SCALES_FROM[i])
                for s in range(4):
                    queue = nc.scalar if i == LAST and s % 2 else nc.sync
                    dram = out_2[g0 : g0 + 2, s:16:4, m0 : m0 + scales.shape[2]]
                    queue.dma_start(
                        out=dram.rearrange("g q m -> q g m").bitcast(I32), in_=scales[s:P:32, :, :].bitcast(I32)
                    )


        jobs = []
        taken = [False] * BANKS
        written = [0]

        def write_jobs():
            while written[0] < len(jobs):
                ready, write = jobs[written[0]]
                b = written[0] % BANKS
                if taken[b] or not ready():
                    break
                written[0] = written[0] + 1
                write(psum.tile([P, GROUP], F32, name="bank%d" % b), b)

        def turn_blocks(c, kp):
            def write(bank, b):
                for s in range(2):
                    for u in range(2):
                        w0 = s * (NB // 2) + kp * (GROUP // 2)
                        if c < HEAD_CHUNKS:
                            pairs = b_sorted[c][:, w0 + u * P : w0 + (u + 1) * P]
                        else:
                            pairs = b_raw[c][:].bitcast(F32)[:, w0 + u : w0 + GROUP // 2 : 2]
                        nc.tensor.transpose(bank[:, (2 * s + u) * P : (2 * s + u + 1) * P], pairs, ident[:])
                key = (c // 2, kp)
                if key not in b_grouped:
                    b_grouped[key] = small_tile([P, 4 * GROUP], BF16)
                half = b_grouped[key][:].bitcast(F32)[:, (c % 2) * GROUP : (c % 2 + 1) * GROUP]
                nc.scalar.copy(
                    out=half.rearrange("p (m su) -> p m su", su=4), in_=bank[:].rearrange("p (su m) -> p m su", su=4)
                )

            return (lambda: c in (b_sorted if c < HEAD_CHUNKS else b_raw), write)

        def multiply(i, a, k):
            rt, jg = k % 2, col0(i) // GROUP + k // 2

            def write(bank, b):
                for kp in range(PASSES):
                    n0 = kp * T * R + a * R + row0(i) + rt * P
                    nc.tensor.matmul_mx(
                        out=bank[:],
                        lhsT=h_words[i % R_UNITS, a][:, kp, rt * P : (rt + 1) * P].bitcast(E5M2X4),
                        lhsT_scale=h_scales[:, n0 : n0 + P],
                        rhs=b_codes[jg, kp][:].bitcast(E4M3X4),
                        rhs_scale=b_scales[jg, kp][:],
                        start=(kp == 0),
                        stop=(kp == PASSES - 1),
                    )
                mx_bank[i, a, k] = (bank, b)
                taken[b] = True

            return (lambda: (jg, PASSES - 1) in b_codes, write)

        def turn_y(i, jl):
            def write(bank, b):
                pairs = y_pairs[i, jl][:].bitcast(F32)
                for rt in row_tiles(i, jl):
                    for u in range(2):
                        nc.tensor.transpose(
                            bank[:, (2 * u + rt) * P : (2 * u + rt + 1) * P],
                            pairs[:, (2 * rt + u) * P : (2 * rt + u + 1) * P],
                            ident[:],
                        )
                rows = slice(row_tiles(i, jl).start * P, UNIT_R)
                nc.scalar.copy(
                    out=y_grouped_tile(i, jl)[:].bitcast(F32).rearrange("p (r u) -> p r u", u=2)[:, rows, :],
                    in_=bank[:].rearrange("p (u r) -> p r u", u=2)[:, rows, :],
                )

            return (lambda: (i, jl) in y_pairs, write)

        def sum_on_tensor(i):
            def write(bank, b):
                terms = (run_wide[i], prod[i, 0], prod[i, 1])
                for t in range(4):
                    cols = slice(t * P, (t + 1) * P)
                    for n, term in enumerate(terms):
                        first, final = n == 0, n == len(terms) - 1
                        nc.tensor.matmul(
                            bank[:, cols], term[:, cols], ident[:], start=first, stop=final, is_transpose=True
                        )
                y_turned[i] = small_tile([P, GROUP], F32)
                nc.scalar.copy(out=y_turned[i][:], in_=bank[:])
                nc.scalar.copy(
                    out=y_grouped_tile(i, 0)[:, 0 : 4 * P].rearrange("p (r t) -> p r t", t=4),
                    in_=bank[:].rearrange("p (t r) -> p r t", t=4),
                )

            return (lambda: (i, 1, 0) in multiplied, write)

        def turn_back(i):
            def write(bank, b):
                for t in range(4):
                    cols = slice(t * P, (t + 1) * P)
                    nc.tensor.transpose(bank[:, cols], y_turned[i][:, cols], ident[:])
                nc.scalar.copy(
                    out=y_tile(i)[:, 0:GROUP].rearrange("r (p t) -> r p t", t=4),
                    in_=bank[:].rearrange("r (t p) -> r p t", t=4),
                )

            return (lambda: i in y_turned, write)

        late_chunks = {place + 1: c for place, c in enumerate(range(HEAD_CHUNKS, J // CHUNK))}
        for c in range(HEAD_CHUNKS):
            jobs.extend(turn_blocks(c, kp) for kp in range(PASSES))
        jobs.extend(multiply(0, 0, k) for k in PIECES)
        jobs.extend(multiply(0, 1, k) for k in PIECES)
        jobs.extend(multiply(1, 0, k) for k in PIECES[:2])
        for i in range(UNITS):
            if i < LAST:
                jobs.extend(multiply(i + 1, 0, k) for k in PIECES[2:])
            if 2 * i in late_chunks:
                jobs.extend(turn_blocks(late_chunks[2 * i], kp) for kp in range(PASSES))
            if i in TENSOR_SUM_UNITS:
                jobs.append(sum_on_tensor(i))
            if i < LAST:
                jobs.extend(multiply(i + 1, 1, k) for k in PIECES[:2])
            if i > 0:
                jobs.extend(turn_y(i - 1, jl) for jl in range(2))
            if 2 * i + 1 in late_chunks:
                jobs.extend(turn_blocks(late_chunks[2 * i + 1], kp) for kp in range(PASSES))
            if i in TENSOR_SUM_UNITS:
                jobs.append(turn_back(i))
            if i < LAST:
                jobs.extend(multiply(i + 1, 1, k) for k in PIECES[2:])
            if i + 1 < LAST:
                jobs.extend(multiply(i + 2, 0, k) for k in PIECES[:2])
        jobs.extend(turn_y(LAST, jl) for jl in (1, 0))


        def sort_blocks(c):
            b_sorted[c] = big_tile([P, NB], F32)
            for kp in range(PASSES):
                nc.vector.tensor_copy(
                    out=b_sorted[c][:].rearrange("m (s g u p) -> m g s u p", s=2, g=PASSES, u=2)[:, kp],
                    in_=b_raw[c][:].bitcast(F32).rearrange("m (s g p u) -> m g s u p", s=2, g=PASSES, u=2)[:, kp],
                )
            write_jobs()

        def quantize_blocks(jg):
            for kp in range(PASSES):
                codes = keep.tile([P, GROUP], U32, name="b_codes%d%d" % (jg, kp), align_bytes=64)
                scales = keep.tile([P, GROUP], U8, name="b_scales%d%d" % (jg, kp), align_bytes=64)
                nc.vector.quantize_mx(out=codes[:].bitcast(E4M3X4), scales=scales[:], in_=b_grouped[jg, kp][:])
                b_codes[jg, kp], b_scales[jg, kp] = codes, scales
            write_jobs()

        def product(i, a, k):
            if k == 0:
                prod[i, a] = ring.tile([P, UNIT], F32, name="prod%d" % a, bufs=2)
            c0 = (k % 2) * UNIT_J + (k // 2) * GROUP
            bank, b = mx_bank[i, a, k]
            dst, src, factor = prod[i, a][:, c0 : c0 + GROUP], bank[:], slope_sb[i, a][:, c0 : c0 + GROUP]
            if i in TENSOR_SUM_UNITS and k == 0:
                dst = dst.rearrange("r (t p) -> r t p", t=4)
                src = src.rearrange("r (p t) -> r t p", t=4)
                factor = factor.rearrange("r (p t) -> r t p", t=4)
            nc.vector.tensor_tensor(out=dst, in0=src, in1=factor, op=MULT)
            multiplied.add((i, a, k))
            taken[b] = False
            write_jobs()

        def widen_run(i):
            run_wide[i] = small_tile([P, GROUP], F32)
            nc.scalar.copy(
                out=run_wide[i][:].rearrange("r (t p) -> r t p", t=4),
                in_=run_sb[i][:, 0:GROUP].rearrange("r (p t) -> r t p", t=4),
            )

        def add_run(engine, i, cols):
            engine.tensor_tensor(out=part[i][:, cols], in0=prod[i, 0][:, cols], in1=run_sb[i][:, cols], op=ADD)

        def add_bin_1(i, cols):
            nc.vector.tensor_tensor(out=y_tile(i)[:, cols], in0=part[i][:, cols], in1=prod[i, 1][:, cols], op=ADD)

        def round_y(i, jl):
            rts = slice(row_tiles(i, jl).start, 2)
            nc.scalar.copy(
                out=y_pairs_tile(i, jl)[:].rearrange("r (rt u p e) -> r rt u p e", rt=2, u=2, e=2)[:, rts],
                in_=group_view(y_sb[i], jl).rearrange("r rt (p u e) -> r rt u p e", u=2, e=2)[:, rts],
            )

        def add_bin_1_rounded(i, jl):
            pairs = y_pairs_tile(i, jl)
            for rt in range(2):
                nc.vector.tensor_tensor(
                    out=pairs[:, rt * GROUP : (rt + 1) * GROUP].rearrange("r (u p e) -> r u p e", u=2, e=2),
                    in0=group_view(part[i], jl)[:, rt, :].rearrange("r (p u e) -> r u p e", u=2, e=2),
                    in1=group_view(prod[i, 1], jl)[:, rt, :].rearrange("r (p u e) -> r u p e", u=2, e=2),
                    op=ADD,
                )
            write_jobs()

        def quantize_y(i, jl):
            c0, s0 = row0(i) - row0(CODES_FROM[i]), row0(i) - row0(SCALES_FROM[i])
            nc.vector.quantize_mx(
                out=y_codes[CODES_FROM[i]][:, jl, c0 : c0 + UNIT_R].bitcast(E4M3X4),
                scales=y_scales[SCALES_FROM[i]][:, jl, s0 : s0 + UNIT_R],
                in_=y_grouped[i, jl][:],
            )
            write_jobs()


        for c in range(HEAD_CHUNKS):
            load_blocks(c)
        load_h_scales()
        for c in range(HEAD_CHUNKS):
            sort_blocks(c)
        load_bin(0, 0)
        load_bin_1_and_run(0)
        for place in range(1, 2 * R_UNITS):
            if place % 2 == 1:
                load_bin((place + 1) // 2, 0)
            else:
                load_bin_1_and_run(place // 2)
            if place in late_chunks:
                load_blocks(late_chunks[place])
        for jg in range(UNIT_J // GROUP):
            quantize_blocks(jg)
        for k in PIECES:
            product(0, 0, k)


        for i in range(UNITS):
            first = GROUP if i in TENSOR_SUM_UNITS else 0
            split = min(UNIT, first + (POOL_COLS_LAST if i == LAST else POOL_COLS))
            part[i] = ring.tile([P, UNIT], F32, name="part", bufs=1)
            add_run(nc.gpsimd, i, slice(first, split))
            for k in PIECES:
                product(i, 1, k)
            if i + 1 in TENSOR_SUM_UNITS:
                widen_run(i + 1)
            if i < LAST:
                for k in PIECES:
                    product(i + 1, 0, k)
            if split < UNIT:
                add_run(nc.vector, i, slice(split, UNIT))
            if i >= QUANTIZE_LAG:
                for jl in range(2):
                    quantize_y(i - QUANTIZE_LAG, jl)
            if 2 * i in late_chunks:
                quantize_blocks(late_chunks[2 * i] // 2)
            if i < LAST:
                add_bin_1(i, slice(first, UNIT))
                for jl in range(2):
                    round_y(i, jl)
                if i + R_UNITS < UNITS:
                    load_bin_1_and_run(i + R_UNITS)
                if i + R_UNITS + 1 < UNITS:
                    load_bin(i + R_UNITS + 1, 0)
            if i >= QUANTIZE_LAG:
                store_planes(i - QUANTIZE_LAG)
            if i < LAST:
                nc.sync.dma_start(out=unit_view(out_0, i), in_=by_row_tile(y_sb[i]))
                write_jobs()


        add_bin_1(LAST, slice(UNIT_J, UNIT))
        round_y(LAST, 0)
        nc.sync.dma_start(out=unit_view(out_0, LAST)[:, 1, :], in_=y_sb[LAST][:, UNIT_J:UNIT])
        add_bin_1_rounded(LAST, 1)
        add_bin_1(LAST, slice(GROUP, UNIT_J))
        nc.sync.dma_start(out=unit_view(out_0, LAST)[:, 0, :], in_=y_sb[LAST][:, 0:UNIT_J])
        for jl in range(2):
            quantize_y(LAST - 1, jl)
        store_planes(LAST - 1)
        for jl in (1, 0):
            quantize_y(LAST, jl)
        store_planes(LAST)
